import numpy as np
import ml_dtypes


def mxq(x, axis, fmt="e4m3"):
    dtype, down = {"e4m3": (ml_dtypes.float8_e4m3fn, 7), "e5m2": (ml_dtypes.float8_e5m2, 14)}[fmt]
    v = np.moveaxis(np.asarray(x, np.float32).astype(ml_dtypes.bfloat16).astype(np.float64), axis, -1)
    blocks = v.reshape(v.shape[:-1] + (-1, 32))
    amax = np.abs(blocks).max(-1, keepdims=True)
    byte = np.maximum(np.where(amax > 0, np.frexp(amax)[1] - 1 + 127, 0) - down, 1)
    scale = np.exp2(byte - 127.0)
    codes = (blocks / scale).astype(np.float32).astype(dtype).astype(np.float64)
    return np.moveaxis((codes * scale).reshape(v.shape), -1, axis)


WIDE = False


def mx_kscale(k):
    if not WIDE:
        return np.ones(k)
    levels = np.array([10, -10, 5, -5, 0])
    if k % 512:
        return np.exp2(np.random.permutation(np.resize(levels, k // 32))).repeat(32)
    a = np.empty((k // 512, 16))
    for p in range(k // 512):
        a[p, :8] = np.random.permutation(np.resize(levels, 8))
        for g in range(8):
            far = levels[np.abs(levels - a[p, g]) >= 10]
            a[p, g + 8] = far[np.random.randint(len(far))]
    return np.exp2(a.ravel()).repeat(32)


def f64(x):
    return np.asarray(x).astype(np.float64)


def striped(idx):
    return np.tile(idx.reshape(-1, 16).T, (8, 1)).astype(np.uint16)


def unstriped(offs):
    return offs[:16].T.reshape(-1).astype(np.int64)


E2M1 = np.array([0.0, 0.5, 1.0, 1.5, 2.0, 3.0, 4.0, 6.0, -0.0, -0.5, -1.0, -1.5, -2.0, -3.0, -4.0, -6.0])


def pack_weight(w, fmt):
    k, n = w.shape
    w = f64(np.asarray(w, np.float32).astype(ml_dtypes.bfloat16)).reshape(k // 32, 32, n)
    amax = np.abs(w).max(1)
    if fmt == "e4m3":
        byte = np.frexp(amax)[1] - 1 + 127 - 7
    else:
        mant, ex = np.frexp(amax / 6.0)
        byte = np.where(mant > 0.5, ex, ex - 1) + 127
    byte = np.clip(np.where(amax > 0, byte, 1), 1, 254)
    scaled = (w * np.exp2(127.0 - byte)[:, None, :]).reshape(k, n).astype(np.float32)
    by_word = np.ascontiguousarray(scaled.reshape(k // 512, 128, 4, n).transpose(0, 1, 3, 2))
    if fmt == "e4m3":
        words = by_word.astype(ml_dtypes.float8_e4m3fn).view(np.uint8)
    else:
        c = by_word.astype(ml_dtypes.float4_e2m1fn).view(np.uint8) & 0xF
        words = (c[..., 0::2] | (c[..., 1::2] << 4)).reshape(k // 512, 128, 2 * n)
    return np.ascontiguousarray(words), np.ascontiguousarray(byte.astype(np.uint8).reshape(k // 512, 16, n))


def unpack_weight(words, scales, fmt):
    g, _, n = scales.shape
    words = np.ascontiguousarray(words).reshape(g, 128, n, -1)
    if fmt == "e4m3":
        vals = words.view(ml_dtypes.float8_e4m3fn).astype(np.float64)
    else:
        nib = np.empty((g, 128, n, 4), np.uint8)
        nib[..., 0::2] = words & 0xF
        nib[..., 1::2] = words >> 4
        vals = E2M1[nib]
    vals = vals * np.repeat(np.exp2(scales.astype(np.float64) - 127.0), 8, axis=1)[..., None]
    return vals.transpose(0, 1, 3, 2).reshape(g * 512, n)


def gelu(v):
    return 0.5 * v * (1.0 + np.tanh(np.sqrt(2.0 / np.pi) * (v + 0.044715 * v**3)))


def striped8(idx):
    return np.concatenate([v.reshape(-1, 16).T for v in idx]).astype(np.uint16)


def unstriped8(offs):
    return np.stack([offs[16 * g:16 * g + 16].T.reshape(-1) for g in range(8)]).astype(np.int64)


def runs(v, idx8):
    k = np.arange(v.shape[0])
    return v[k[:, None], idx8[k % 512 // 64]]


K, K2, H, N, T, S, T2 = 1024, 512, 512, 384, 2048, 1024, 2048

def setup_inputs():
    n = np.random.standard_normal
    s, s2, u = mx_kscale(K)[:, None], mx_kscale(K2)[:, None], mx_kscale(H)[:, None]
    tab_words, tab_scales = pack_weight(n((K, T)) * s, "e4m3")
    tab2_words, tab2_scales = pack_weight(n((K2, T)) * s2, "e4m3")
    w1 = (n((K, H)) / s * 0.6 / np.sqrt(K)).astype(np.float32)
    w2_words, w2_scales = pack_weight(n((K2, H)) / s2 * 1.5 / np.sqrt(K2), "e2m1")
    w3_words, w3_scales = pack_weight(n((H, N)) / u * 0.75 / np.sqrt(H), "e2m1")
    w4 = (n((H, N)) / u * 1.9 / np.sqrt(H)).astype(np.float32)
    gm = (np.exp(0.4 * n(H)) * u[:, 0]).astype(np.float32)
    gs = (np.exp(0.4 * n(H)) * u[:, 0]).astype(np.float32)
    page1 = (0.6 * n((N, T2))).astype(np.float32)
    wgo = np.exp(0.3 * n((128, S))).astype(np.float32)
    offs = striped8(np.stack([np.random.permutation(T)[:S] for _ in range(8)]))
    offs2 = striped(np.random.permutation(T)[:S])
    offs3 = striped(np.random.permutation(T2)[:S])
    return dict(tab_words=tab_words, tab_scales=tab_scales, tab2_words=tab2_words, tab2_scales=tab2_scales,
                w1=w1, w2_words=w2_words, w2_scales=w2_scales, w3_words=w3_words, w3_scales=w3_scales,
                w4=w4, gm=gm, gs=gs, page1=page1, wgo=wgo, offs=offs, offs2=offs2, offs3=offs3)

def reference(tab_words, tab_scales, tab2_words, tab2_scales, w1, w2_words, w2_scales, w3_words, w3_scales,
              w4, gm, gs, page1, wgo, offs, offs2, offs3):
    v = runs(unpack_weight(tab_words, tab_scales, "e4m3"), unstriped8(offs))
    v2 = unpack_weight(tab2_words, tab2_scales, "e4m3")[:, unstriped(offs2)]
    b = mxq(f64(w1), 0, "e4m3").T @ v
    q = np.tanh(unpack_weight(w2_words, w2_scales, "e2m1").T @ v2)
    z1 = np.maximum(b, q) * f64(gm)[:, None]
    z2 = np.sin(b * q) * f64(gs)[:, None]
    y = (unpack_weight(w3_words, w3_scales, "e2m1").T @ mxq(z1, 0, "e4m3")
              + mxq(f64(w4), 0, "e4m3").T @ mxq(z2, 0, "e4m3"))
    out = f64(page1).copy()
    out[:, unstriped(offs3)] = np.tile(f64(wgo), (N // 128, 1)) * y
    return out

@@ -1,0 +1,226 @@
+import math
+from contextlib import ExitStack
+
+import concourse.mybir as mybir
+
+K, K2, H, N, T, S, T2 = 1024, 512, 512, 384, 2048, 1024, 2048
+FLOPS = 2 * S * (K * H + K2 * H + 2 * H * N)
+
+F32 = mybir.dt.float32
+BF16 = mybir.dt.bfloat16
+I32 = mybir.dt.int32
+U32 = mybir.dt.uint32
+U16 = mybir.dt.uint16
+U8 = mybir.dt.uint8
+FP8X4 = mybir.dt.float8_e4m3fn_x4
+FP4X4 = mybir.dt.float4_e2m1fn_x4
+ALU = mybir.AluOpType
+ACT = mybir.ActivationFunctionType
+
+P = 128
+PACK = 4
+CHUNK = 256
+HALF = 512
+PLANE = 8
+SLOT = 8192
+ROUNDER = 1.5 * 2.0**23
+
+
+def tile_list_sample_clearance_features_kernel(
+    tc, tab_words, tab_scales, tab2_words, tab2_scales, w1, w2_words, w2_scales, w3_words, w3_scales,
+    w4, gm, gs, page1, wgo, offs, offs2, offs3, out,
+):
+    nc = tc.nc
+    n_chunks = S // CHUNK
+    n_tiles = N // P
+    with ExitStack() as ctx:
+        keep = ctx.enter_context(tc.tile_pool(name="keep", bufs=1))
+        shared = ctx.enter_context(tc.tile_pool(name="shared", bufs=1))
+        work = ctx.enter_context(tc.tile_pool(name="work", bufs=4))
+        ps_bq = ctx.enter_context(tc.psum_pool(name="ps_bq", bufs=4))
+        ps_y = ctx.enter_context(tc.psum_pool(name="ps_y", bufs=2))
+
+        def kept(shape, dtype, name):
+            return keep.tile(shape, dtype, name=name, align_bytes=64)
+
+        def placed(shape, dtype, name, offset):
+            return shared.tile(shape, dtype, name=name, offset=offset, align_bytes=64)
+
+        def load_rows(queue, plane, rows):
+            for d in range(4):
+                queue.dma_start(out=plane[32 * d : 32 * d + 4, :].bitcast(I32), in_=rows[4 * d : 4 * d + 4, :].bitcast(I32))
+
+        list1 = kept([P, S // 16], U16, "list1")
+        list2 = kept([P, S // 16], U16, "list2")
+        list3 = kept([P, S // 16], U16, "list3")
+        tab_sc = placed([P, T], U8, "tab_sc", 0)
+        tab2_sc = placed([P, T], U8, "tab2_sc", 4 * SLOT)
+        w2_sc_raw = placed([P, H], U8, "w2_sc_raw", 5 * SLOT)
+        w2_raw = placed([P, 2 * H], U8, "w2_raw", 5 * SLOT + H)
+        for plane in (tab_sc, tab2_sc, w2_sc_raw):
+            nc.vector.memset(plane[:].bitcast(I32), 0)
+
+        for lst, src in ((list1, offs), (list2, offs2), (list3, offs3)):
+            nc.sync.dma_start(lst[:], src)
+        nc.sync.dma_start(out=w2_raw[:].bitcast(I32), in_=w2_words[0].bitcast(I32))
+        by_parity = tab_scales.rearrange("a (g e) t -> e g a t", e=2)
+        for e in range(2):
+            nc.gpsimd.dma_start(out=tab_sc[e:P:PLANE, :].bitcast(I32), in_=by_parity[e].bitcast(I32))
+        load_rows(nc.scalar, tab2_sc, tab2_scales[0])
+        load_rows(nc.gpsimd, w2_sc_raw, w2_scales[0])
+
+        w1_raw = [placed([P, PACK, H], F32, "w1_raw%d" % a, (1 + a) * SLOT) for a in range(2)]
+        tab2_w = placed([P, T], U32, "tab2_w", 3 * SLOT)
+        tab_w = [kept([P, T], U32, "tab_w0"), placed([P, T], U32, "tab_w1", 0)]
+        for a in range(2):
+            nc.sync.dma_start(out=w1_raw[a][:], in_=w1[512 * a : 512 * (a + 1), :].rearrange("(p j) c -> p j c", j=PACK))
+        nc.sync.dma_start(out=tab2_w[:].bitcast(I32), in_=tab2_words[0].rearrange("p t i -> p (t i)").bitcast(I32))
+
+        def load_tab_words(a):
+            nc.sync.dma_start(out=tab_w[a][:].bitcast(I32), in_=tab_words[a].rearrange("p t i -> p (t i)").bitcast(I32))
+
+        load_tab_words(0)
+
+        v_sc_picked = kept([P, S], U8, "v_sc_picked")
+        nc.vector.tensor_copy(v_sc_picked[:], tab_sc[:].indirect(list1[:]))
+        load_tab_words(1)
+        v_sc = kept([P, S], U8, "v_sc")
+        nc.vector.tensor_copy(v_sc[:].bitcast(I32), v_sc_picked[:].bitcast(I32))
+        for a in range(2):
+            for e in range(2):
+                row = PLANE * a + e
+                nc.gpsimd.dma_start(out=v_sc[row + 2 : P : 32, :].bitcast(I32), in_=v_sc_picked[row + 16 : P : 32, :].bitcast(I32))
+        v2_sc = kept([P, S], U8, "v2_sc")
+        nc.vector.tensor_copy(v2_sc[:], tab2_sc[:].indirect(list2[:]))
+
+        gm_sb = placed([P, PACK], F32, "gm_sb", 4 * SLOT)
+        gs_sb = placed([P, PACK], F32, "gs_sb", 4 * SLOT + 64)
+        w3_w = placed([P, 2 * N], U8, "w3_w", 4 * SLOT + 128)
+        w4_raw = placed([P, PACK, N], F32, "w4_raw", 4 * SLOT + 1024)
+        nc.sync.dma_start(out=gm_sb[:], in_=gm.rearrange("(p t) -> p t", t=PACK))
+        nc.sync.dma_start(out=gs_sb[:], in_=gs.rearrange("(p t) -> p t", t=PACK))
+        nc.sync.dma_start(out=w4_raw[:], in_=w4.rearrange("(p j) n -> p j n", j=PACK))
+        nc.sync.dma_start(out=w3_w[:].bitcast(I32), in_=w3_words[0].bitcast(I32))
+
+        w2_w = kept([P, 2 * H], U8, "w2_w")
+        nc.vector.tensor_copy(out=w2_w[:].rearrange("p (t m e) -> p t m e", t=PACK, e=2),
+                              in_=w2_raw[:].rearrange("p (m t e) -> p t m e", t=PACK, e=2))
+        w2_sc = kept([P, H], U8, "w2_sc")
+        nc.vector.tensor_copy(out=w2_sc[:].rearrange("p (t m) -> p t m", t=PACK),
+                              in_=w2_sc_raw[:].rearrange("p (m t) -> p t m", t=PACK))
+
+        w3_sc = placed([P, N], U8, "w3_sc", 5 * SLOT)
+        nc.vector.memset(w3_sc[:].bitcast(I32), 0)
+        load_rows(nc.sync, w3_sc, w3_scales[0])
+        wgo_sb = placed([P, S], F32, "wgo_sb", 5 * SLOT + H)
+        nc.sync.dma_start(out=wgo_sb[:], in_=wgo)
+
+        w1_codes, w1_sc = [], []
+        for a in range(2):
+            w1_bf = kept([P, PACK * H], BF16, "w1_bf%d" % a)
+            nc.scalar.copy(out=w1_bf[:].rearrange("p (t m j) -> p m t j", t=PACK, j=PACK),
+                           in_=w1_raw[a][:].rearrange("p j (m t) -> p m t j", t=PACK))
+            w1_codes.append(kept([P, H], U32, "w1_codes%d" % a))
+            w1_sc.append(kept([P, H], U8, "w1_sc%d" % a))
+            nc.vector.quantize_mx(out=w1_codes[a][:].bitcast(FP8X4), scales=w1_sc[a][:], in_=w1_bf[:])
+
+        def pick_words(table, lst, name):
+            halves = []
+            for h in range(S // HALF):
+                picked = kept([P, HALF], U32, "%s_%d" % (name, h))
+                nc.vector.tensor_copy(picked[:], table[:].indirect(lst[:, h * HALF // 16 : (h + 1) * HALF // 16]))
+                halves.append(picked)
+            return halves
+
+        def chunk_words(halves, c):
+            h, c0 = divmod(c * CHUNK, HALF)
+            return halves[h][:, c0 : c0 + CHUNK].bitcast(FP8X4)
+
+        v2_w = pick_words(tab2_w, list2, "v2_w")
+        q_sb = []
+        for c in range(n_chunks):
+            cols = slice(c * CHUNK, (c + 1) * CHUNK)
+            q_sb.append(kept([P, PACK * CHUNK], F32, "q%d" % c))
+            for u in range(2):
+                bank = ps_bq.tile([P, 2 * CHUNK], F32, name="bq_bank")
+                for e in range(2):
+                    t = 2 * u + e
+                    nc.tensor.matmul_mx(out=bank[:, e * CHUNK : (e + 1) * CHUNK],
+                                        lhsT=w2_w[:, 2 * P * t : 2 * P * (t + 1)].bitcast(FP4X4),
+                                        lhsT_scale=w2_sc[:, P * t : P * (t + 1)],
+                                        rhs=chunk_words(v2_w, c), rhs_scale=v2_sc[:, cols], start=True, stop=True)
+                nc.scalar.activation(q_sb[c][:, 2 * CHUNK * u : 2 * CHUNK * (u + 1)], bank[:], ACT.Tanh)
+
+        pages = [placed([P, T2], F32, "page%d" % i, (1 + i) * SLOT) for i in range(n_tiles)]
+        for i in range(n_tiles):
+            nc.sync.dma_start(out=pages[i][:], in_=page1[P * i : P * (i + 1), :])
+
+        v_w = [pick_words(tab_w[a], list1, "v_w%d" % a) for a in range(2)]
+
+        w4_bf = kept([P, N * PACK], BF16, "w4_bf")
+        nc.scalar.copy(out=w4_bf[:].rearrange("p (n j) -> p n j", j=PACK), in_=w4_raw[:].rearrange("p j n -> p n j"))
+        w4_codes = kept([P, N], U32, "w4_codes")
+        w4_sc = kept([P, N], U8, "w4_sc")
+        nc.vector.quantize_mx(out=w4_codes[:].bitcast(FP8X4), scales=w4_sc[:], in_=w4_bf[:])
+
+        def wide(dtype, name):
+            return work.tile([P, PACK * CHUNK], dtype, name=name, align_bytes=64)
+
+        def scale_round_quantise(values, gain, name):
+            planar = wide(BF16, name + "_planar")
+            for t in range(PACK):
+                cols = slice(t * CHUNK, (t + 1) * CHUNK)
+                nc.scalar.activation(planar[:, cols], values[:, cols], ACT.Copy, scale=gain[:, t : t + 1])
+            woven = wide(BF16, name + "_woven")
+            nc.scalar.copy(out=woven[:].rearrange("p (n t) -> p n t", t=PACK), in_=planar[:].rearrange("p (t n) -> p n t", t=PACK))
+            codes = work.tile([P, CHUNK], U32, name=name + "_codes", align_bytes=64)
+            scales = work.tile([P, CHUNK], U8, name=name + "_sc", align_bytes=64)
+            nc.vector.quantize_mx(out=codes[:].bitcast(FP8X4), scales=scales[:], in_=woven[:])
+            return codes, scales
+
+        for c in range(n_chunks):
+            cols = slice(c * CHUNK, (c + 1) * CHUNK)
+            turns = wide(F32, "turns")
+            larger = wide(F32, "larger")
+            for u in range(2):
+                bank = ps_bq.tile([P, 2 * CHUNK], F32, name="bq_bank")
+                for e in range(2):
+                    t = 2 * u + e
+                    for a in range(2):
+                        nc.tensor.matmul_mx(out=bank[:, e * CHUNK : (e + 1) * CHUNK],
+                                            lhsT=w1_codes[a][:, P * t : P * (t + 1)].bitcast(FP8X4),
+                                            lhsT_scale=w1_sc[a][:, P * t : P * (t + 1)],
+                                            rhs=chunk_words(v_w[a], c), rhs_scale=v_sc[PLANE * a :, cols],
+                                            start=(a == 0), stop=(a == 1))
+                part = slice(2 * CHUNK * u, 2 * CHUNK * (u + 1))
+                nc.vector.scalar_tensor_tensor(out=turns[:, part], in0=bank[:], scalar=1.0 / (2.0 * math.pi),
+                                               in1=q_sb[c][:, part], op0=ALU.mult, op1=ALU.mult)
+                nc.vector.tensor_tensor(out=larger[:, part], in0=bank[:], in1=q_sb[c][:, part], op=ALU.max)
+            whole = wide(I32, "whole")
+            nc.vector.tensor_scalar(out=whole[:], in0=turns[:], scalar1=ROUNDER, scalar2=None, op0=ALU.add)
+            rest = wide(F32, "rest")
+            nc.vector.scalar_tensor_tensor(out=rest[:], in0=whole[:], scalar=ROUNDER, in1=turns[:],
+                                           op0=ALU.subtract, op1=ALU.subtract)
+            z1_codes, z1_sc = scale_round_quantise(larger, gm_sb, "z1")
+            sines = wide(F32, "sines")
+            nc.scalar.activation(sines[:], rest[:], ACT.Sin, scale=-2.0 * math.pi)
+            z2_codes, z2_sc = scale_round_quantise(sines, gs_sb, "z2")
+
+            y_banks = [ps_y.tile([P, 2 * CHUNK], F32, name="y_bank0"), ps_y.tile([P, CHUNK], F32, name="y_bank1")]
+            y_sb = work.tile([P, n_tiles * CHUNK], F32, name="y_sb")
+            for i in range(n_tiles):
+                acc = y_banks[i // 2][:, (i % 2) * CHUNK : (i % 2 + 1) * CHUNK]
+                nc.tensor.matmul_mx(out=acc, lhsT=w3_w[:, 2 * P * i : 2 * P * (i + 1)].bitcast(FP4X4),
+                                    lhsT_scale=w3_sc[:, P * i : P * (i + 1)],
+                                    rhs=z1_codes[:].bitcast(FP8X4), rhs_scale=z1_sc[:], start=True, stop=False)
+                nc.tensor.matmul_mx(out=acc, lhsT=w4_codes[:, P * i : P * (i + 1)].bitcast(FP8X4),
+                                    lhsT_scale=w4_sc[:, P * i : P * (i + 1)],
+                                    rhs=z2_codes[:].bitcast(FP8X4), rhs_scale=z2_sc[:], start=False, stop=True)
+            nc.scalar.copy(out=y_sb[:, : 2 * CHUNK], in_=y_banks[0][:])
+            nc.scalar.copy(out=y_sb[:, 2 * CHUNK :], in_=y_banks[1][:])
+            for i in range(n_tiles):
+                nc.vector.tensor_tensor(out=pages[i][:].indirect(list3[:, c * CHUNK // 16 : (c + 1) * CHUNK // 16]),
+                                        in0=y_sb[:, i * CHUNK : (i + 1) * CHUNK], in1=wgo_sb[:, cols], op=ALU.mult)
+
+        for i in range(n_tiles):
+            nc.sync.dma_start(out=out[P * i : P * (i + 1), :], in_=pages[i][:])

@@ -36,7 +36,7 @@ def tile_list_sample_clearance_features_kernel(
     with ExitStack() as ctx:
         keep = ctx.enter_context(tc.tile_pool(name="keep", bufs=1))
         shared = ctx.enter_context(tc.tile_pool(name="shared", bufs=1))
-        work = ctx.enter_context(tc.tile_pool(name="work", bufs=4))
+        work = ctx.enter_context(tc.tile_pool(name="work", bufs=2))
         ps_bq = ctx.enter_context(tc.psum_pool(name="ps_bq", bufs=4))
         ps_y = ctx.enter_context(tc.psum_pool(name="ps_y", bufs=2))
 
@@ -46,57 +46,60 @@ def tile_list_sample_clearance_features_kernel(
         def placed(shape, dtype, name, offset):
             return shared.tile(shape, dtype, name=name, offset=offset, align_bytes=64)
 
-        def load_rows(queue, plane, rows):
+        def load_rows(plane, rows):
+            words = rows.shape[1] // 4
             for d in range(4):
-                queue.dma_start(out=plane[32 * d : 32 * d + 4, :].bitcast(I32), in_=rows[4 * d : 4 * d + 4, :].bitcast(I32))
+                four = rows[4 * d : 4 * d + 4, :].bitcast(I32)
+                nc.sync.dma_start(out=plane[32 * d : 32 * d + 32, :].bitcast(I32), in_=four.unsqueeze(0).to_broadcast([8, 4, words]))
 
         list1 = kept([P, S // 16], U16, "list1")
         list2 = kept([P, S // 16], U16, "list2")
         list3 = kept([P, S // 16], U16, "list3")
-        tab_sc = placed([P, T], U8, "tab_sc", 0)
-        tab2_sc = placed([P, T], U8, "tab2_sc", 4 * SLOT)
-        w2_sc_raw = placed([P, H], U8, "w2_sc_raw", 5 * SLOT)
-        w2_raw = placed([P, 2 * H], U8, "w2_raw", 5 * SLOT + H)
-        for plane in (tab_sc, tab2_sc, w2_sc_raw):
-            nc.vector.memset(plane[:].bitcast(I32), 0)
+        tab_sc = kept([P, T], U8, "tab_sc")
+        tab2_sc = placed([P, T], U8, "tab2_sc", 3 * SLOT)
+        w2_sc_raw = placed([P, H], U8, "w2_sc_raw", 4 * SLOT)
+        w2_raw = placed([P, 2 * H], U8, "w2_raw", 4 * SLOT + H)
+        w1_raw = [kept([P, PACK, H], F32, "w1_raw0"), placed([P, PACK, H], F32, "w1_raw1", 2 * SLOT)]
+        tab2_w = kept([P, T], U32, "tab2_w")
+        tab_w = [placed([P, T], U32, "tab_w%d" % a, a * SLOT) for a in range(2)]
 
-        for lst, src in ((list1, offs), (list2, offs2), (list3, offs3)):
-            nc.sync.dma_start(lst[:], src)
-        nc.sync.dma_start(out=w2_raw[:].bitcast(I32), in_=w2_words[0].bitcast(I32))
+        def load_words(table, words):
+            nc.sync.dma_start(out=table[:].bitcast(I32), in_=words.rearrange("p t i -> p (t i)").bitcast(I32))
+
+        def load_w1(a):
+            nc.sync.dma_start(out=w1_raw[a][:], in_=w1[512 * a : 512 * (a + 1), :].rearrange("(p j) c -> p j c", j=PACK))
+
+        nc.vector.memset(tab_sc[:].bitcast(I32), 0)
         by_parity = tab_scales.rearrange("a (g e) t -> e g a t", e=2)
         for e in range(2):
-            nc.gpsimd.dma_start(out=tab_sc[e:P:PLANE, :].bitcast(I32), in_=by_parity[e].bitcast(I32))
-        load_rows(nc.scalar, tab2_sc, tab2_scales[0])
-        load_rows(nc.gpsimd, w2_sc_raw, w2_scales[0])
-
-        w1_raw = [placed([P, PACK, H], F32, "w1_raw%d" % a, (1 + a) * SLOT) for a in range(2)]
-        tab2_w = placed([P, T], U32, "tab2_w", 3 * SLOT)
-        tab_w = [kept([P, T], U32, "tab_w0"), placed([P, T], U32, "tab_w1", 0)]
-        for a in range(2):
-            nc.sync.dma_start(out=w1_raw[a][:], in_=w1[512 * a : 512 * (a + 1), :].rearrange("(p j) c -> p j c", j=PACK))
-        nc.sync.dma_start(out=tab2_w[:].bitcast(I32), in_=tab2_words[0].rearrange("p t i -> p (t i)").bitcast(I32))
-
-        def load_tab_words(a):
-            nc.sync.dma_start(out=tab_w[a][:].bitcast(I32), in_=tab_words[a].rearrange("p t i -> p (t i)").bitcast(I32))
-
-        load_tab_words(0)
+            nc.scalar.dma_start(out=tab_sc[e:P:PLANE, :].bitcast(I32), in_=by_parity[e].bitcast(I32))
+        nc.sync.dma_start(list1[:], offs)
+        nc.sync.dma_start(list2[:], offs2)
+        load_words(tab2_w, tab2_words[0])
+        load_rows(tab2_sc, tab2_scales[0])
+        load_w1(0)
+        nc.sync.dma_start(out=w2_raw[:].bitcast(I32), in_=w2_words[0].bitcast(I32))
+        load_rows(w2_sc_raw, w2_scales[0])
+        load_w1(1)
+        load_words(tab_w[0], tab_words[0])
+        nc.sync.dma_start(list3[:], offs3)
+        load_words(tab_w[1], tab_words[1])
 
         v_sc_picked = kept([P, S], U8, "v_sc_picked")
         nc.vector.tensor_copy(v_sc_picked[:], tab_sc[:].indirect(list1[:]))
-        load_tab_words(1)
         v_sc = kept([P, S], U8, "v_sc")
         nc.vector.tensor_copy(v_sc[:].bitcast(I32), v_sc_picked[:].bitcast(I32))
         for a in range(2):
             for e in range(2):
                 row = PLANE * a + e
-                nc.gpsimd.dma_start(out=v_sc[row + 2 : P : 32, :].bitcast(I32), in_=v_sc_picked[row + 16 : P : 32, :].bitcast(I32))
+                nc.sync.dma_start(out=v_sc[row + 2 : P : 32, :].bitcast(I32), in_=v_sc_picked[row + 16 : P : 32, :].bitcast(I32))
         v2_sc = kept([P, S], U8, "v2_sc")
         nc.vector.tensor_copy(v2_sc[:], tab2_sc[:].indirect(list2[:]))
 
-        gm_sb = placed([P, PACK], F32, "gm_sb", 4 * SLOT)
-        gs_sb = placed([P, PACK], F32, "gs_sb", 4 * SLOT + 64)
-        w3_w = placed([P, 2 * N], U8, "w3_w", 4 * SLOT + 128)
-        w4_raw = placed([P, PACK, N], F32, "w4_raw", 4 * SLOT + 1024)
+        gm_sb = placed([P, PACK], F32, "gm_sb", 3 * SLOT)
+        gs_sb = placed([P, PACK], F32, "gs_sb", 3 * SLOT + 64)
+        w3_w = placed([P, 2 * N], U8, "w3_w", 3 * SLOT + 128)
+        w4_raw = placed([P, PACK, N], F32, "w4_raw", 3 * SLOT + 1024)
         nc.sync.dma_start(out=gm_sb[:], in_=gm.rearrange("(p t) -> p t", t=PACK))
         nc.sync.dma_start(out=gs_sb[:], in_=gs.rearrange("(p t) -> p t", t=PACK))
         nc.sync.dma_start(out=w4_raw[:], in_=w4.rearrange("(p j) n -> p j n", j=PACK))
@@ -109,10 +112,9 @@ def tile_list_sample_clearance_features_kernel(
         nc.vector.tensor_copy(out=w2_sc[:].rearrange("p (t m) -> p t m", t=PACK),
                               in_=w2_sc_raw[:].rearrange("p (m t) -> p t m", t=PACK))
 
-        w3_sc = placed([P, N], U8, "w3_sc", 5 * SLOT)
-        nc.vector.memset(w3_sc[:].bitcast(I32), 0)
-        load_rows(nc.sync, w3_sc, w3_scales[0])
-        wgo_sb = placed([P, S], F32, "wgo_sb", 5 * SLOT + H)
+        w3_sc = placed([P, N], U8, "w3_sc", 4 * SLOT)
+        load_rows(w3_sc, w3_scales[0])
+        wgo_sb = placed([P, S], F32, "wgo_sb", 4 * SLOT + H)
         nc.sync.dma_start(out=wgo_sb[:], in_=wgo)
 
         w1_codes, w1_sc = [], []
@@ -151,11 +153,11 @@ def tile_list_sample_clearance_features_kernel(
                                         rhs=chunk_words(v2_w, c), rhs_scale=v2_sc[:, cols], start=True, stop=True)
                 nc.scalar.activation(q_sb[c][:, 2 * CHUNK * u : 2 * CHUNK * (u + 1)], bank[:], ACT.Tanh)
 
-        pages = [placed([P, T2], F32, "page%d" % i, (1 + i) * SLOT) for i in range(n_tiles)]
+        v_w = [pick_words(tab_w[a], list1, "v_w%d" % a) for a in range(2)]
+
+        pages = [placed([P, T2], F32, "page%d" % i, i * SLOT) for i in range(n_tiles)]
         for i in range(n_tiles):
             nc.sync.dma_start(out=pages[i][:], in_=page1[P * i : P * (i + 1), :])
-
-        v_w = [pick_words(tab_w[a], list1, "v_w%d" % a) for a in range(2)]
 
         w4_bf = kept([P, N * PACK], BF16, "w4_bf")
         nc.scalar.copy(out=w4_bf[:].rearrange("p (n j) -> p n j", j=PACK), in_=w4_raw[:].rearrange("p j n -> p n j"))
@@ -163,11 +165,10 @@ def tile_list_sample_clearance_features_kernel(
         w4_sc = kept([P, N], U8, "w4_sc")
         nc.vector.quantize_mx(out=w4_codes[:].bitcast(FP8X4), scales=w4_sc[:], in_=w4_bf[:])
 
-        def wide(dtype, name):
-            return work.tile([P, PACK * CHUNK], dtype, name=name, align_bytes=64)
+        def wide(dtype, name, bufs=2):
+            return work.tile([P, PACK * CHUNK], dtype, name=name, align_bytes=64, bufs=bufs)
 
-        def scale_round_quantise(values, gain, name):
-            planar = wide(BF16, name + "_planar")
+        def scale_round_quantise(values, gain, planar, name):
             for t in range(PACK):
                 cols = slice(t * CHUNK, (t + 1) * CHUNK)
                 nc.scalar.activation(planar[:, cols], values[:, cols], ACT.Copy, scale=gain[:, t : t + 1])
@@ -178,10 +179,10 @@ def tile_list_sample_clearance_features_kernel(
             nc.vector.quantize_mx(out=codes[:].bitcast(FP8X4), scales=scales[:], in_=woven[:])
             return codes, scales
 
-        for c in range(n_chunks):
+        def features(c):
             cols = slice(c * CHUNK, (c + 1) * CHUNK)
             turns = wide(F32, "turns")
-            larger = wide(F32, "larger")
+            larger = wide(F32, "larger", bufs=n_chunks)
             for u in range(2):
                 bank = ps_bq.tile([P, 2 * CHUNK], F32, name="bq_bank")
                 for e in range(2):
@@ -198,16 +199,16 @@ def tile_list_sample_clearance_features_kernel(
                 nc.vector.tensor_tensor(out=larger[:, part], in0=bank[:], in1=q_sb[c][:, part], op=ALU.max)
             whole = wide(I32, "whole")
             nc.vector.tensor_scalar(out=whole[:], in0=turns[:], scalar1=ROUNDER, scalar2=None, op0=ALU.add)
-            rest = wide(F32, "rest")
+            rest = wide(F32, "rest", bufs=n_chunks)
             nc.vector.scalar_tensor_tensor(out=rest[:], in0=whole[:], scalar=ROUNDER, in1=turns[:],
                                            op0=ALU.subtract, op1=ALU.subtract)
-            z1_codes, z1_sc = scale_round_quantise(larger, gm_sb, "z1")
+            z1_codes, z1_sc = scale_round_quantise(larger, gm_sb, wide(BF16, "z1_planar"), "z1")
             sines = wide(F32, "sines")
             nc.scalar.activation(sines[:], rest[:], ACT.Sin, scale=-2.0 * math.pi)
-            z2_codes, z2_sc = scale_round_quantise(sines, gs_sb, "z2")
+            z2_planar = keep.tile([P, PACK * CHUNK], BF16, name="z2_planar", tag="relay%d" % c)
+            z2_codes, z2_sc = scale_round_quantise(sines, gs_sb, z2_planar, "z2")
 
             y_banks = [ps_y.tile([P, 2 * CHUNK], F32, name="y_bank0"), ps_y.tile([P, CHUNK], F32, name="y_bank1")]
-            y_sb = work.tile([P, n_tiles * CHUNK], F32, name="y_sb")
             for i in range(n_tiles):
                 acc = y_banks[i // 2][:, (i % 2) * CHUNK : (i % 2 + 1) * CHUNK]
                 nc.tensor.matmul_mx(out=acc, lhsT=w3_w[:, 2 * P * i : 2 * P * (i + 1)].bitcast(FP4X4),
@@ -216,11 +217,30 @@ def tile_list_sample_clearance_features_kernel(
                 nc.tensor.matmul_mx(out=acc, lhsT=w4_codes[:, P * i : P * (i + 1)].bitcast(FP8X4),
                                     lhsT_scale=w4_sc[:, P * i : P * (i + 1)],
                                     rhs=z2_codes[:].bitcast(FP8X4), rhs_scale=z2_sc[:], start=False, stop=True)
-            nc.scalar.copy(out=y_sb[:, : 2 * CHUNK], in_=y_banks[0][:])
-            nc.scalar.copy(out=y_sb[:, 2 * CHUNK :], in_=y_banks[1][:])
-            for i in range(n_tiles):
-                nc.vector.tensor_tensor(out=pages[i][:].indirect(list3[:, c * CHUNK // 16 : (c + 1) * CHUNK // 16]),
-                                        in0=y_sb[:, i * CHUNK : (i + 1) * CHUNK], in1=wgo_sb[:, cols], op=ALU.mult)
+            return y_banks
+
+        y_last = [kept([P, 2 * CHUNK], F32, "y_last%d" % h) for h in range(n_chunks // 2)]
+
+        def scatter(i, values, first, count):
+            nc.vector.tensor_tensor(out=pages[i][:].indirect(list3[:, first // 16 : (first + count) // 16]),
+                                    in0=values, in1=wgo_sb[:, first : first + count], op=ALU.mult)
+
+        def place(c, y_banks):
+            y_sb = keep.tile([P, 2 * CHUNK], F32, name="y_sb", tag="relay%d" % (c + 1))
+            nc.scalar.copy(out=y_sb[:], in_=y_banks[0][:])
+            pair, second = divmod(c, 2)
+            nc.scalar.copy(out=y_last[pair][:, second * CHUNK : (second + 1) * CHUNK], in_=y_banks[1][:])
+            for i in range(2):
+                scatter(i, y_sb[:, i * CHUNK : (i + 1) * CHUNK], c * CHUNK, CHUNK)
+            if second:
+                scatter(2, y_last[pair][:], pair * 2 * CHUNK, 2 * CHUNK)
+
+        waiting = features(0)
+        for c in range(1, n_chunks):
+            coming = features(c)
+            place(c - 1, waiting)
+            waiting = coming
+        place(n_chunks - 1, waiting)
 
         for i in range(n_tiles):
             nc.sync.dma_start(out=out[P * i : P * (i + 1), :], in_=pages[i][:])

@@ -56,11 +56,11 @@ def tile_list_sample_clearance_features_kernel(
         list2 = kept([P, S // 16], U16, "list2")
         list3 = kept([P, S // 16], U16, "list3")
         tab_sc = kept([P, T], U8, "tab_sc")
-        tab2_sc = placed([P, T], U8, "tab2_sc", 3 * SLOT)
+        tab2_sc = kept([P, T], U8, "tab2_sc")
         w2_sc_raw = placed([P, H], U8, "w2_sc_raw", 4 * SLOT)
         w2_raw = placed([P, 2 * H], U8, "w2_raw", 4 * SLOT + H)
-        w1_raw = [kept([P, PACK, H], F32, "w1_raw0"), placed([P, PACK, H], F32, "w1_raw1", 2 * SLOT)]
-        tab2_w = kept([P, T], U32, "tab2_w")
+        w1_raw = [placed([P, PACK, H], F32, "w1_raw0", 2 * SLOT), placed([P, PACK, H], F32, "w1_raw1", 5 * SLOT)]
+        tab2_w = placed([P, T], U32, "tab2_w", 3 * SLOT)
         tab_w = [placed([P, T], U32, "tab_w%d" % a, a * SLOT) for a in range(2)]
 
         def load_words(table, words):
@@ -73,11 +73,11 @@ def tile_list_sample_clearance_features_kernel(
         by_parity = tab_scales.rearrange("a (g e) t -> e g a t", e=2)
         for e in range(2):
             nc.scalar.dma_start(out=tab_sc[e:P:PLANE, :].bitcast(I32), in_=by_parity[e].bitcast(I32))
-        nc.sync.dma_start(list1[:], offs)
         nc.sync.dma_start(list2[:], offs2)
-        load_words(tab2_w, tab2_words[0])
         load_rows(tab2_sc, tab2_scales[0])
         load_w1(0)
+        nc.sync.dma_start(list1[:], offs)
+        load_words(tab2_w, tab2_words[0])
         nc.sync.dma_start(out=w2_raw[:].bitcast(I32), in_=w2_words[0].bitcast(I32))
         load_rows(w2_sc_raw, w2_scales[0])
         load_w1(1)
@@ -85,6 +85,8 @@ def tile_list_sample_clearance_features_kernel(
         nc.sync.dma_start(list3[:], offs3)
         load_words(tab_w[1], tab_words[1])
 
+        v2_sc = kept([P, S], U8, "v2_sc")
+        nc.vector.tensor_copy(v2_sc[:], tab2_sc[:].indirect(list2[:]))
         v_sc_picked = kept([P, S], U8, "v_sc_picked")
         nc.vector.tensor_copy(v_sc_picked[:], tab_sc[:].indirect(list1[:]))
         v_sc = kept([P, S], U8, "v_sc")
@@ -93,23 +95,12 @@ def tile_list_sample_clearance_features_kernel(
             for e in range(2):
                 row = PLANE * a + e
                 nc.sync.dma_start(out=v_sc[row + 2 : P : 32, :].bitcast(I32), in_=v_sc_picked[row + 16 : P : 32, :].bitcast(I32))
-        v2_sc = kept([P, S], U8, "v2_sc")
-        nc.vector.tensor_copy(v2_sc[:], tab2_sc[:].indirect(list2[:]))
-
-        gm_sb = placed([P, PACK], F32, "gm_sb", 3 * SLOT)
-        gs_sb = placed([P, PACK], F32, "gs_sb", 3 * SLOT + 64)
-        w3_w = placed([P, 2 * N], U8, "w3_w", 3 * SLOT + 128)
-        w4_raw = placed([P, PACK, N], F32, "w4_raw", 3 * SLOT + 1024)
-        nc.sync.dma_start(out=gm_sb[:], in_=gm.rearrange("(p t) -> p t", t=PACK))
-        nc.sync.dma_start(out=gs_sb[:], in_=gs.rearrange("(p t) -> p t", t=PACK))
-        nc.sync.dma_start(out=w4_raw[:], in_=w4.rearrange("(p j) n -> p j n", j=PACK))
-        nc.sync.dma_start(out=w3_w[:].bitcast(I32), in_=w3_words[0].bitcast(I32))
 
         w2_w = kept([P, 2 * H], U8, "w2_w")
-        nc.vector.tensor_copy(out=w2_w[:].rearrange("p (t m e) -> p t m e", t=PACK, e=2),
+        nc.gpsimd.tensor_copy(out=w2_w[:].rearrange("p (t m e) -> p t m e", t=PACK, e=2),
                               in_=w2_raw[:].rearrange("p (m t e) -> p t m e", t=PACK, e=2))
         w2_sc = kept([P, H], U8, "w2_sc")
-        nc.vector.tensor_copy(out=w2_sc[:].rearrange("p (t m) -> p t m", t=PACK),
+        nc.gpsimd.tensor_copy(out=w2_sc[:].rearrange("p (t m) -> p t m", t=PACK),
                               in_=w2_sc_raw[:].rearrange("p (m t) -> p t m", t=PACK))
 
         w3_sc = placed([P, N], U8, "w3_sc", 4 * SLOT)
@@ -139,12 +130,21 @@ def tile_list_sample_clearance_features_kernel(
             return halves[h][:, c0 : c0 + CHUNK].bitcast(FP8X4)
 
         v2_w = pick_words(tab2_w, list2, "v2_w")
+        gm_sb = placed([P, PACK], F32, "gm_sb", 3 * SLOT)
+        gs_sb = placed([P, PACK], F32, "gs_sb", 3 * SLOT + 64)
+        w3_w = placed([P, 2 * N], U8, "w3_w", 3 * SLOT + 128)
+        w4_raw = placed([P, PACK, N], F32, "w4_raw", 3 * SLOT + 1024)
+        nc.sync.dma_start(out=gm_sb[:], in_=gm.rearrange("(p t) -> p t", t=PACK))
+        nc.sync.dma_start(out=gs_sb[:], in_=gs.rearrange("(p t) -> p t", t=PACK))
+        nc.sync.dma_start(out=w4_raw[:], in_=w4.rearrange("(p j) n -> p j n", j=PACK))
+        nc.sync.dma_start(out=w3_w[:].bitcast(I32), in_=w3_words[0].bitcast(I32))
+
         q_sb = []
         for c in range(n_chunks):
             cols = slice(c * CHUNK, (c + 1) * CHUNK)
-            q_sb.append(kept([P, PACK * CHUNK], F32, "q%d" % c))
+            q_sb.append(placed([P, PACK * CHUNK], F32, "q%d" % c, 5 * SLOT + c * SLOT // 2))
             for u in range(2):
-                bank = ps_bq.tile([P, 2 * CHUNK], F32, name="bq_bank")
+                bank = ps_y.tile([P, 2 * CHUNK], F32, name="y_bank%d" % u)
                 for e in range(2):
                     t = 2 * u + e
                     nc.tensor.matmul_mx(out=bank[:, e * CHUNK : (e + 1) * CHUNK],
@@ -160,7 +160,7 @@ def tile_list_sample_clearance_features_kernel(
             nc.sync.dma_start(out=pages[i][:], in_=page1[P * i : P * (i + 1), :])
 
         w4_bf = kept([P, N * PACK], BF16, "w4_bf")
-        nc.scalar.copy(out=w4_bf[:].rearrange("p (n j) -> p n j", j=PACK), in_=w4_raw[:].rearrange("p j n -> p n j"))
+        nc.scalar.copy(out=w4_bf[:].rearrange("p (c i j) -> p c j i", j=PACK, i=4), in_=w4_raw[:].rearrange("p j (c i) -> p c j i", i=4))
         w4_codes = kept([P, N], U32, "w4_codes")
         w4_sc = kept([P, N], U8, "w4_sc")
         nc.vector.quantize_mx(out=w4_codes[:].bitcast(FP8X4), scales=w4_sc[:], in_=w4_bf[:])
@@ -173,7 +173,7 @@ def tile_list_sample_clearance_features_kernel(
                 cols = slice(t * CHUNK, (t + 1) * CHUNK)
                 nc.scalar.activation(planar[:, cols], values[:, cols], ACT.Copy, scale=gain[:, t : t + 1])
             woven = wide(BF16, name + "_woven")
-            nc.scalar.copy(out=woven[:].rearrange("p (n t) -> p n t", t=PACK), in_=planar[:].rearrange("p (t n) -> p n t", t=PACK))
+            nc.scalar.copy(out=woven[:].rearrange("p (c i t) -> p c t i", t=PACK, i=4), in_=planar[:].rearrange("p (t c i) -> p c t i", t=PACK, i=4))
             codes = work.tile([P, CHUNK], U32, name=name + "_codes", align_bytes=64)
             scales = work.tile([P, CHUNK], U8, name=name + "_sc", align_bytes=64)
             nc.vector.quantize_mx(out=codes[:].bitcast(FP8X4), scales=scales[:], in_=woven[:])
@@ -198,7 +198,7 @@ def tile_list_sample_clearance_features_kernel(
                                                in1=q_sb[c][:, part], op0=ALU.mult, op1=ALU.mult)
                 nc.vector.tensor_tensor(out=larger[:, part], in0=bank[:], in1=q_sb[c][:, part], op=ALU.max)
             whole = wide(I32, "whole")
-            nc.vector.tensor_scalar(out=whole[:], in0=turns[:], scalar1=ROUNDER, scalar2=None, op0=ALU.add)
+            nc.gpsimd.tensor_scalar(out=whole[:], in0=turns[:], scalar1=1.0, scalar2=ROUNDER, op0=ALU.mult, op1=ALU.add)
             rest = wide(F32, "rest", bufs=n_chunks)
             nc.vector.scalar_tensor_tensor(out=rest[:], in0=whole[:], scalar=ROUNDER, in1=turns[:],
                                            op0=ALU.subtract, op1=ALU.subtract)

@@ -20,7 +20,6 @@ ACT = mybir.ActivationFunctionType
 P = 128
 PACK = 4
 CHUNK = 256
-HALF = 512
 PLANE = 8
 SLOT = 8192
 ROUNDER = 1.5 * 2.0**23
@@ -46,11 +45,9 @@ def tile_list_sample_clearance_features_kernel(
         def placed(shape, dtype, name, offset):
             return shared.tile(shape, dtype, name=name, offset=offset, align_bytes=64)
 
-        def load_rows(plane, rows):
-            words = rows.shape[1] // 4
-            for d in range(4):
-                four = rows[4 * d : 4 * d + 4, :].bitcast(I32)
-                nc.sync.dma_start(out=plane[32 * d : 32 * d + 32, :].bitcast(I32), in_=four.unsqueeze(0).to_broadcast([8, 4, words]))
+        def load_rows(plane, rows, quadrants):
+            for d in quadrants:
+                nc.sync.dma_start(out=plane[32 * d : 32 * d + 4, :].bitcast(I32), in_=rows[4 * d : 4 * d + 4, :].bitcast(I32))
 
         list1 = kept([P, S // 16], U16, "list1")
         list2 = kept([P, S // 16], U16, "list2")
@@ -69,24 +66,24 @@ def tile_list_sample_clearance_features_kernel(
         def load_w1(a):
             nc.sync.dma_start(out=w1_raw[a][:], in_=w1[512 * a : 512 * (a + 1), :].rearrange("(p j) c -> p j c", j=PACK))
 
-        nc.vector.memset(tab_sc[:].bitcast(I32), 0)
+        for plane in (tab_sc, tab2_sc, w2_sc_raw):
+            nc.vector.memset(plane[:].bitcast(I32), 0)
         by_parity = tab_scales.rearrange("a (g e) t -> e g a t", e=2)
         for e in range(2):
             nc.scalar.dma_start(out=tab_sc[e:P:PLANE, :].bitcast(I32), in_=by_parity[e].bitcast(I32))
-        nc.sync.dma_start(list2[:], offs2)
-        load_rows(tab2_sc, tab2_scales[0])
-        load_w1(0)
         nc.sync.dma_start(list1[:], offs)
+        load_w1(0)
+        nc.sync.dma_start(list2[:], offs2)
+        load_rows(tab2_sc, tab2_scales[0], range(3))
         load_words(tab2_w, tab2_words[0])
-        nc.sync.dma_start(out=w2_raw[:].bitcast(I32), in_=w2_words[0].bitcast(I32))
-        load_rows(w2_sc_raw, w2_scales[0])
+        load_rows(tab2_sc, tab2_scales[0], range(3, 4))
         load_w1(1)
+        nc.sync.dma_start(out=w2_raw[:].bitcast(I32), in_=w2_words[0].bitcast(I32))
+        load_rows(w2_sc_raw, w2_scales[0], range(4))
         load_words(tab_w[0], tab_words[0])
         nc.sync.dma_start(list3[:], offs3)
         load_words(tab_w[1], tab_words[1])
 
-        v2_sc = kept([P, S], U8, "v2_sc")
-        nc.vector.tensor_copy(v2_sc[:], tab2_sc[:].indirect(list2[:]))
         v_sc_picked = kept([P, S], U8, "v_sc_picked")
         nc.vector.tensor_copy(v_sc_picked[:], tab_sc[:].indirect(list1[:]))
         v_sc = kept([P, S], U8, "v_sc")
@@ -104,7 +101,8 @@ def tile_list_sample_clearance_features_kernel(
                               in_=w2_sc_raw[:].rearrange("p (m t) -> p t m", t=PACK))
 
         w3_sc = placed([P, N], U8, "w3_sc", 4 * SLOT)
-        load_rows(w3_sc, w3_scales[0])
+        nc.gpsimd.memset(w3_sc[:].bitcast(I32), 0)
+        load_rows(w3_sc, w3_scales[0], range(4))
         wgo_sb = placed([P, S], F32, "wgo_sb", 4 * SLOT + H)
         nc.sync.dma_start(out=wgo_sb[:], in_=wgo)
 
@@ -117,19 +115,15 @@ def tile_list_sample_clearance_features_kernel(
             w1_sc.append(kept([P, H], U8, "w1_sc%d" % a))
             nc.vector.quantize_mx(out=w1_codes[a][:].bitcast(FP8X4), scales=w1_sc[a][:], in_=w1_bf[:])
 
-        def pick_words(table, lst, name):
-            halves = []
-            for h in range(S // HALF):
-                picked = kept([P, HALF], U32, "%s_%d" % (name, h))
-                nc.vector.tensor_copy(picked[:], table[:].indirect(lst[:, h * HALF // 16 : (h + 1) * HALF // 16]))
-                halves.append(picked)
-            return halves
+        def pick_words(table, lst, piece, name):
+            chunks = []
+            for first in range(0, S, piece):
+                picked = kept([P, piece], U32, "%s_%d" % (name, first))
+                nc.vector.tensor_copy(picked[:], table[:].indirect(lst[:, first // 16 : (first + piece) // 16]))
+                chunks.extend(picked[:, c0 : c0 + CHUNK].bitcast(FP8X4) for c0 in range(0, piece, CHUNK))
+            return chunks
 
-        def chunk_words(halves, c):
-            h, c0 = divmod(c * CHUNK, HALF)
-            return halves[h][:, c0 : c0 + CHUNK].bitcast(FP8X4)
-
-        v2_w = pick_words(tab2_w, list2, "v2_w")
+        v2_w = pick_words(tab2_w, list2, S, "v2_w")
         gm_sb = placed([P, PACK], F32, "gm_sb", 3 * SLOT)
         gs_sb = placed([P, PACK], F32, "gs_sb", 3 * SLOT + 64)
         w3_w = placed([P, 2 * N], U8, "w3_w", 3 * SLOT + 128)
@@ -139,6 +133,8 @@ def tile_list_sample_clearance_features_kernel(
         nc.sync.dma_start(out=w4_raw[:], in_=w4.rearrange("(p j) n -> p j n", j=PACK))
         nc.sync.dma_start(out=w3_w[:].bitcast(I32), in_=w3_words[0].bitcast(I32))
 
+        v2_sc = kept([P, S], U8, "v2_sc")
+        nc.vector.tensor_copy(v2_sc[:], tab2_sc[:].indirect(list2[:]))
         q_sb = []
         for c in range(n_chunks):
             cols = slice(c * CHUNK, (c + 1) * CHUNK)
@@ -150,17 +146,17 @@ def tile_list_sample_clearance_features_kernel(
                     nc.tensor.matmul_mx(out=bank[:, e * CHUNK : (e + 1) * CHUNK],
                                         lhsT=w2_w[:, 2 * P * t : 2 * P * (t + 1)].bitcast(FP4X4),
                                         lhsT_scale=w2_sc[:, P * t : P * (t + 1)],
-                                        rhs=chunk_words(v2_w, c), rhs_scale=v2_sc[:, cols], start=True, stop=True)
+                                        rhs=v2_w[c], rhs_scale=v2_sc[:, cols], start=True, stop=True)
                 nc.scalar.activation(q_sb[c][:, 2 * CHUNK * u : 2 * CHUNK * (u + 1)], bank[:], ACT.Tanh)
 
-        v_w = [pick_words(tab_w[a], list1, "v_w%d" % a) for a in range(2)]
+        v_w = [pick_words(tab_w[0], list1, S, "v_w0"), pick_words(tab_w[1], list1, CHUNK, "v_w1")]
 
         pages = [placed([P, T2], F32, "page%d" % i, i * SLOT) for i in range(n_tiles)]
         for i in range(n_tiles):
             nc.sync.dma_start(out=pages[i][:], in_=page1[P * i : P * (i + 1), :])
 
         w4_bf = kept([P, N * PACK], BF16, "w4_bf")
-        nc.scalar.copy(out=w4_bf[:].rearrange("p (c i j) -> p c j i", j=PACK, i=4), in_=w4_raw[:].rearrange("p j (c i) -> p c j i", i=4))
+        nc.gpsimd.tensor_copy(out=w4_bf[:].rearrange("p (n j) -> p n j", j=PACK), in_=w4_raw[:].rearrange("p j n -> p n j"))
         w4_codes = kept([P, N], U32, "w4_codes")
         w4_sc = kept([P, N], U8, "w4_sc")
         nc.vector.quantize_mx(out=w4_codes[:].bitcast(FP8X4), scales=w4_sc[:], in_=w4_bf[:])
@@ -191,7 +187,7 @@ def tile_list_sample_clearance_features_kernel(
                         nc.tensor.matmul_mx(out=bank[:, e * CHUNK : (e + 1) * CHUNK],
                                             lhsT=w1_codes[a][:, P * t : P * (t + 1)].bitcast(FP8X4),
                                             lhsT_scale=w1_sc[a][:, P * t : P * (t + 1)],
-                                            rhs=chunk_words(v_w[a], c), rhs_scale=v_sc[PLANE * a :, cols],
+                                            rhs=v_w[a][c], rhs_scale=v_sc[PLANE * a :, cols],
                                             start=(a == 0), stop=(a == 1))
                 part = slice(2 * CHUNK * u, 2 * CHUNK * (u + 1))
                 nc.vector.scalar_tensor_tensor(out=turns[:, part], in0=bank[:], scalar=1.0 / (2.0 * math.pi),

import math
from contextlib import ExitStack

import concourse.mybir as mybir

K, K2, H, N, T, S, T2 = 1024, 512, 512, 384, 2048, 1024, 2048
FLOPS = 2 * S * (K * H + K2 * H + 2 * H * N)

F32 = mybir.dt.float32
BF16 = mybir.dt.bfloat16
I32 = mybir.dt.int32
U32 = mybir.dt.uint32
U16 = mybir.dt.uint16
U8 = mybir.dt.uint8
FP8X4 = mybir.dt.float8_e4m3fn_x4
FP4X4 = mybir.dt.float4_e2m1fn_x4
ALU = mybir.AluOpType
ACT = mybir.ActivationFunctionType

P = 128
PACK = 4
CHUNK = 256
PLANE = 8
SLOT = 8192
ROUNDER = 1.5 * 2.0**23


def tile_list_sample_clearance_features_kernel(
    tc, tab_words, tab_scales, tab2_words, tab2_scales, w1, w2_words, w2_scales, w3_words, w3_scales,
    w4, gm, gs, page1, wgo, offs, offs2, offs3, out,
):
    nc = tc.nc
    n_chunks = S // CHUNK
    n_tiles = N // P
    with ExitStack() as ctx:
        keep = ctx.enter_context(tc.tile_pool(name="keep", bufs=1))
        shared = ctx.enter_context(tc.tile_pool(name="shared", bufs=1))
        work = ctx.enter_context(tc.tile_pool(name="work", bufs=2))
        ps_bq = ctx.enter_context(tc.psum_pool(name="ps_bq", bufs=4))
        ps_y = ctx.enter_context(tc.psum_pool(name="ps_y", bufs=2))

        def kept(shape, dtype, name):
            return keep.tile(shape, dtype, name=name, align_bytes=64)

        def placed(shape, dtype, name, offset):
            return shared.tile(shape, dtype, name=name, offset=offset, align_bytes=64)

        def load_rows(plane, rows, quadrants):
            for d in quadrants:
                nc.sync.dma_start(out=plane[32 * d : 32 * d + 4, :].bitcast(I32), in_=rows[4 * d : 4 * d + 4, :].bitcast(I32))

        list1 = kept([P, S // 16], U16, "list1")
        list2 = kept([P, S // 16], U16, "list2")
        list3 = kept([P, S // 16], U16, "list3")
        tab_sc = kept([P, T], U8, "tab_sc")
        tab2_sc = kept([P, T], U8, "tab2_sc")
        w2_sc_raw = placed([P, H], U8, "w2_sc_raw", 4 * SLOT)
        w2_raw = placed([P, 2 * H], U8, "w2_raw", 4 * SLOT + H)
        w1_raw = [placed([P, PACK, H], F32, "w1_raw0", 2 * SLOT), placed([P, PACK, H], F32, "w1_raw1", 5 * SLOT)]
        tab2_w = placed([P, T], U32, "tab2_w", 3 * SLOT)
        tab_w = [placed([P, T], U32, "tab_w%d" % a, a * SLOT) for a in range(2)]

        def load_words(table, words):
            nc.sync.dma_start(out=table[:].bitcast(I32), in_=words.rearrange("p t i -> p (t i)").bitcast(I32))

        def load_w1(a):
            nc.sync.dma_start(out=w1_raw[a][:], in_=w1[512 * a : 512 * (a + 1), :].rearrange("(p j) c -> p j c", j=PACK))

        for plane in (tab_sc, tab2_sc, w2_sc_raw):
            nc.vector.memset(plane[:].bitcast(I32), 0)
        by_parity = tab_scales.rearrange("a (g e) t -> e g a t", e=2)
        for e in range(2):
            nc.scalar.dma_start(out=tab_sc[e:P:PLANE, :].bitcast(I32), in_=by_parity[e].bitcast(I32))
        nc.sync.dma_start(list1[:], offs)
        load_w1(0)
        nc.sync.dma_start(list2[:], offs2)
        load_rows(tab2_sc, tab2_scales[0], range(3))
        load_words(tab2_w, tab2_words[0])
        load_rows(tab2_sc, tab2_scales[0], range(3, 4))
        load_w1(1)
        nc.sync.dma_start(out=w2_raw[:].bitcast(I32), in_=w2_words[0].bitcast(I32))
        load_rows(w2_sc_raw, w2_scales[0], range(4))
        load_words(tab_w[0], tab_words[0])
        nc.sync.dma_start(list3[:], offs3)
        load_words(tab_w[1], tab_words[1])

        v_sc_picked = kept([P, S], U8, "v_sc_picked")
        nc.vector.tensor_copy(v_sc_picked[:], tab_sc[:].indirect(list1[:]))
        v_sc = kept([P, S], U8, "v_sc")
        nc.vector.tensor_copy(v_sc[:].bitcast(I32), v_sc_picked[:].bitcast(I32))
        for a in range(2):
            for e in range(2):
                row = PLANE * a + e
                nc.sync.dma_start(out=v_sc[row + 2 : P : 32, :].bitcast(I32), in_=v_sc_picked[row + 16 : P : 32, :].bitcast(I32))

        w2_w = kept([P, 2 * H], U8, "w2_w")
        nc.gpsimd.tensor_copy(out=w2_w[:].rearrange("p (t m e) -> p t m e", t=PACK, e=2),
                              in_=w2_raw[:].rearrange("p (m t e) -> p t m e", t=PACK, e=2))
        w2_sc = kept([P, H], U8, "w2_sc")
        nc.gpsimd.tensor_copy(out=w2_sc[:].rearrange("p (t m) -> p t m", t=PACK),
                              in_=w2_sc_raw[:].rearrange("p (m t) -> p t m", t=PACK))

        w3_sc = placed([P, N], U8, "w3_sc", 4 * SLOT)
        nc.gpsimd.memset(w3_sc[:].bitcast(I32), 0)
        load_rows(w3_sc, w3_scales[0], range(4))
        wgo_sb = placed([P, S], F32, "wgo_sb", 4 * SLOT + H)
        nc.sync.dma_start(out=wgo_sb[:], in_=wgo)

        w1_codes, w1_sc = [], []
        for a in range(2):
            w1_bf = kept([P, PACK * H], BF16, "w1_bf%d" % a)
            nc.scalar.copy(out=w1_bf[:].rearrange("p (t m j) -> p m t j", t=PACK, j=PACK),
                           in_=w1_raw[a][:].rearrange("p j (m t) -> p m t j", t=PACK))
            w1_codes.append(kept([P, H], U32, "w1_codes%d" % a))
            w1_sc.append(kept([P, H], U8, "w1_sc%d" % a))
            nc.vector.quantize_mx(out=w1_codes[a][:].bitcast(FP8X4), scales=w1_sc[a][:], in_=w1_bf[:])

        def pick_words(table, lst, piece, name):
            chunks = []
            for first in range(0, S, piece):
                picked = kept([P, piece], U32, "%s_%d" % (name, first))
                nc.vector.tensor_copy(picked[:], table[:].indirect(lst[:, first // 16 : (first + piece) // 16]))
                chunks.extend(picked[:, c0 : c0 + CHUNK].bitcast(FP8X4) for c0 in range(0, piece, CHUNK))
            return chunks

        v2_w = pick_words(tab2_w, list2, S, "v2_w")
        gm_sb = placed([P, PACK], F32, "gm_sb", 3 * SLOT)
        gs_sb = placed([P, PACK], F32, "gs_sb", 3 * SLOT + 64)
        w3_w = placed([P, 2 * N], U8, "w3_w", 3 * SLOT + 128)
        w4_raw = placed([P, PACK, N], F32, "w4_raw", 3 * SLOT + 1024)
        nc.sync.dma_start(out=gm_sb[:], in_=gm.rearrange("(p t) -> p t", t=PACK))
        nc.sync.dma_start(out=gs_sb[:], in_=gs.rearrange("(p t) -> p t", t=PACK))
        nc.sync.dma_start(out=w4_raw[:], in_=w4.rearrange("(p j) n -> p j n", j=PACK))
        nc.sync.dma_start(out=w3_w[:].bitcast(I32), in_=w3_words[0].bitcast(I32))

        v2_sc = kept([P, S], U8, "v2_sc")
        nc.vector.tensor_copy(v2_sc[:], tab2_sc[:].indirect(list2[:]))
        q_sb = []
        for c in range(n_chunks):
            cols = slice(c * CHUNK, (c + 1) * CHUNK)
            q_sb.append(placed([P, PACK * CHUNK], F32, "q%d" % c, 5 * SLOT + c * SLOT // 2))
            for u in range(2):
                bank = ps_y.tile([P, 2 * CHUNK], F32, name="y_bank%d" % u)
                for e in range(2):
                    t = 2 * u + e
                    nc.tensor.matmul_mx(out=bank[:, e * CHUNK : (e + 1) * CHUNK],
                                        lhsT=w2_w[:, 2 * P * t : 2 * P * (t + 1)].bitcast(FP4X4),
                                        lhsT_scale=w2_sc[:, P * t : P * (t + 1)],
                                        rhs=v2_w[c], rhs_scale=v2_sc[:, cols], start=True, stop=True)
                nc.scalar.activation(q_sb[c][:, 2 * CHUNK * u : 2 * CHUNK * (u + 1)], bank[:], ACT.Tanh)

        v_w = [pick_words(tab_w[0], list1, S, "v_w0"), pick_words(tab_w[1], list1, CHUNK, "v_w1")]

        pages = [placed([P, T2], F32, "page%d" % i, i * SLOT) for i in range(n_tiles)]
        for i in range(n_tiles):
            nc.sync.dma_start(out=pages[i][:], in_=page1[P * i : P * (i + 1), :])

        w4_bf = kept([P, N * PACK], BF16, "w4_bf")
        nc.gpsimd.tensor_copy(out=w4_bf[:].rearrange("p (n j) -> p n j", j=PACK), in_=w4_raw[:].rearrange("p j n -> p n j"))
        w4_codes = kept([P, N], U32, "w4_codes")
        w4_sc = kept([P, N], U8, "w4_sc")
        nc.vector.quantize_mx(out=w4_codes[:].bitcast(FP8X4), scales=w4_sc[:], in_=w4_bf[:])

        def wide(dtype, name, bufs=2):
            return work.tile([P, PACK * CHUNK], dtype, name=name, align_bytes=64, bufs=bufs)

        def scale_round_quantise(values, gain, planar, name):
            for t in range(PACK):
                cols = slice(t * CHUNK, (t + 1) * CHUNK)
                nc.scalar.activation(planar[:, cols], values[:, cols], ACT.Copy, scale=gain[:, t : t + 1])
            woven = wide(BF16, name + "_woven")
            nc.scalar.copy(out=woven[:].rearrange("p (c i t) -> p c t i", t=PACK, i=4), in_=planar[:].rearrange("p (t c i) -> p c t i", t=PACK, i=4))
            codes = work.tile([P, CHUNK], U32, name=name + "_codes", align_bytes=64)
            scales = work.tile([P, CHUNK], U8, name=name + "_sc", align_bytes=64)
            nc.vector.quantize_mx(out=codes[:].bitcast(FP8X4), scales=scales[:], in_=woven[:])
            return codes, scales

        def features(c):
            cols = slice(c * CHUNK, (c + 1) * CHUNK)
            turns = wide(F32, "turns")
            larger = wide(F32, "larger", bufs=n_chunks)
            for u in range(2):
                bank = ps_bq.tile([P, 2 * CHUNK], F32, name="bq_bank")
                for e in range(2):
                    t = 2 * u + e
                    for a in range(2):
                        nc.tensor.matmul_mx(out=bank[:, e * CHUNK : (e + 1) * CHUNK],
                                            lhsT=w1_codes[a][:, P * t : P * (t + 1)].bitcast(FP8X4),
                                            lhsT_scale=w1_sc[a][:, P * t : P * (t + 1)],
                                            rhs=v_w[a][c], rhs_scale=v_sc[PLANE * a :, cols],
                                            start=(a == 0), stop=(a == 1))
                part = slice(2 * CHUNK * u, 2 * CHUNK * (u + 1))
                nc.vector.scalar_tensor_tensor(out=turns[:, part], in0=bank[:], scalar=1.0 / (2.0 * math.pi),
                                               in1=q_sb[c][:, part], op0=ALU.mult, op1=ALU.mult)
                nc.vector.tensor_tensor(out=larger[:, part], in0=bank[:], in1=q_sb[c][:, part], op=ALU.max)
            whole = wide(I32, "whole")
            nc.gpsimd.tensor_scalar(out=whole[:], in0=turns[:], scalar1=1.0, scalar2=ROUNDER, op0=ALU.mult, op1=ALU.add)
            rest = wide(F32, "rest", bufs=n_chunks)
            nc.vector.scalar_tensor_tensor(out=rest[:], in0=whole[:], scalar=ROUNDER, in1=turns[:],
                                           op0=ALU.subtract, op1=ALU.subtract)
            z1_codes, z1_sc = scale_round_quantise(larger, gm_sb, wide(BF16, "z1_planar"), "z1")
            sines = wide(F32, "sines")
            nc.scalar.activation(sines[:], rest[:], ACT.Sin, scale=-2.0 * math.pi)
            z2_planar = keep.tile([P, PACK * CHUNK], BF16, name="z2_planar", tag="relay%d" % c)
            z2_codes, z2_sc = scale_round_quantise(sines, gs_sb, z2_planar, "z2")

            y_banks = [ps_y.tile([P, 2 * CHUNK], F32, name="y_bank0"), ps_y.tile([P, CHUNK], F32, name="y_bank1")]
            for i in range(n_tiles):
                acc = y_banks[i // 2][:, (i % 2) * CHUNK : (i % 2 + 1) * CHUNK]
                nc.tensor.matmul_mx(out=acc, lhsT=w3_w[:, 2 * P * i : 2 * P * (i + 1)].bitcast(FP4X4),
                                    lhsT_scale=w3_sc[:, P * i : P * (i + 1)],
                                    rhs=z1_codes[:].bitcast(FP8X4), rhs_scale=z1_sc[:], start=True, stop=False)
                nc.tensor.matmul_mx(out=acc, lhsT=w4_codes[:, P * i : P * (i + 1)].bitcast(FP8X4),
                                    lhsT_scale=w4_sc[:, P * i : P * (i + 1)],
                                    rhs=z2_codes[:].bitcast(FP8X4), rhs_scale=z2_sc[:], start=False, stop=True)
            return y_banks

        y_last = [kept([P, 2 * CHUNK], F32, "y_last%d" % h) for h in range(n_chunks // 2)]

        def scatter(i, values, first, count):
            nc.vector.tensor_tensor(out=pages[i][:].indirect(list3[:, first // 16 : (first + count) // 16]),
                                    in0=values, in1=wgo_sb[:, first : first + count], op=ALU.mult)

        def place(c, y_banks):
            y_sb = keep.tile([P, 2 * CHUNK], F32, name="y_sb", tag="relay%d" % (c + 1))
            nc.scalar.copy(out=y_sb[:], in_=y_banks[0][:])
            pair, second = divmod(c, 2)
            nc.scalar.copy(out=y_last[pair][:, second * CHUNK : (second + 1) * CHUNK], in_=y_banks[1][:])
            for i in range(2):
                scatter(i, y_sb[:, i * CHUNK : (i + 1) * CHUNK], c * CHUNK, CHUNK)
            if second:
                scatter(2, y_last[pair][:], pair * 2 * CHUNK, 2 * CHUNK)

        waiting = features(0)
        for c in range(1, n_chunks):
            coming = features(c)
            place(c - 1, waiting)
            waiting = coming
        place(n_chunks - 1, waiting)

        for i in range(n_tiles):
            nc.sync.dma_start(out=out[P * i : P * (i + 1), :], in_=pages[i][:])
